import numpy as np
CORES = [33,161,289,417,57,185,313,441]
N = 8
F = 128
BOUND = 271.5
def setup_inputs(rng):
    gr = rng.standard_normal((1, 128, N * F), dtype=np.float32) + rng.standard_normal((N, 128, N * F), dtype=np.float32)
    gr = gr * (2.0 ** rng.uniform(-3, 3, (1, 128, 1))).astype(np.float32)
    return {"gr": gr}
def setup_inputs_big(rng):
    d = setup_inputs(rng)
    for k in ("gr",): d[k] = (d[k].astype(np.float32) * 1024.0).astype(d[k].dtype)
    return d
def setup_inputs_small(rng):
    d = setup_inputs(rng)
    for k in ("gr",): d[k] = (d[k].astype(np.float32) * (1 / 1024.0)).astype(d[k].dtype)
    return d
def setup_inputs_apart(rng):
    d = setup_inputs(rng)
    f = (10.0 ** rng.permutation(np.linspace(-1.5, 1.5, N))).astype(np.float32).reshape(N, 1, 1)
    for k in ("gr",): d[k] = (d[k].astype(np.float32) * f).astype(d[k].dtype)
    return d
def setup_inputs_mixed(rng):
    d = setup_inputs(rng)
    f = (10.0 ** rng.uniform(-3, 3, (1, 128, 1))).astype(np.float32); shape = rng.integers(2, size=(1, 128, 1))
    for k in ("gr",):
        x = d[k].astype(np.float32)
        other = x * np.where(rng.random((1, 128, N * F)) < 0.5, 0.1, 1.0).astype(np.float32)
        d[k] = (np.where(shape == 1, other, x) * f).astype(d[k].dtype)
    return d
def reference(gr):
    s = gr.astype(np.float64).sum(axis=0)
    nrm = np.sqrt((s ** 2).sum(axis=1, keepdims=True))
    s = s * np.minimum(1.0, BOUND / nrm)
    return {"y": np.stack([s[:, F * r:F * r + F] for r in range(N)]).astype(np.float32)}

@@ -1,0 +1,203 @@
+from concourse.bass import DstId, RemoteDMATransfer
+from concourse.mybir import AluOpType, ActivationFunctionType
+
+F = 128
+SIM_CORES = 512
+
+SCRATCH = {
+    "gb": ("sbuf", [128, 8 * F], "float32"),
+    "rx": ("sbuf", [128, 5 * F], "float32"),
+    "tx": ("sbuf", [128, 2 * F], "float32"),
+    "nb": ("sbuf", [128, 8], "float32"),
+    "sm": ("sbuf", [128, 24], "float32"),
+    "yo": ("sbuf", [128, F], "float32"),
+    "acc": ("psum", [128, F], "float32"),
+}
+SEMAPHORES = ["ld1", "ld2", "ld3", "ld4", "sent", "in_b", "in_c", "in_ka", "in_kb", "in_n", "k_in", "k_n",
+              "vc", "vd", "va", "sq", "vx", "sr", "vy", "st"]
+
+_PLAN = {}
+
+
+def _plan(T, topo):
+    if _PLAN:
+        return _PLAN
+    ranks = [int(u) for u in T.cores]
+    for t in ranks:
+        col = [u for u in ranks if u != t and topo.chip(u) == topo.chip(t)]
+        b = [u for u in col if topo.same_plane(t, u)][0]
+        c = [u for u in col if topo.may_write(t, u) and not topo.same_plane(t, u)][0]
+        d = [u for u in col if not topo.may_write(t, u)][0]
+        a = [u for u in ranks if u != t and topo.host(u) == topo.host(t)][0]
+        k = [x for x in range(SIM_CORES)
+             if x != t and topo.host(x) == topo.host(t) and topo.chip(x) == topo.chip(t)
+             and topo.die(x) == topo.die(t) and topo.may_write(x, a)][0]
+        _PLAN[t] = {"a": a, "b": b, "c": c, "d": d, "k": k}
+    return _PLAN
+
+
+def _bits(m):
+    return [1 << i for i in range(m.bit_length()) if (m >> i) & 1]
+
+
+def _n(m):
+    return len(_bits(m))
+
+
+def _dst(topo, dst, src):
+    rid, pid = topo.addr(dst, src)
+    return DstId(rid=rid, pnc=pid)
+
+
+def _blk(buf, j, n=1):
+    return buf[:, j * F:(j + n) * F]
+
+
+def _helper(g, core, u, T, topo, P):
+    rk = T.rank_of
+    S = T.sem
+    a, b = P[u]["a"], P[u]["b"]
+    ab = P[b]["a"]
+    pair = sorted([rk(a), rk(ab)])
+    n_own = _n(topo.mask(u, core) & ~topo.mask(u, P[u]["c"]))
+    n_cab = _n(topo.mask(P[u]["c"], core)) // 2
+    g.vector.wait_ge(S.k_in, n_own + n_cab)
+    g.vector.tensor_tensor(T.tx[:, 0:2 * F], T.gb[:, 0:2 * F], T.gb[:, 2 * F:4 * F], AluOpType.add).then_inc(S.vd, 1)
+    g.wait_ge(S.vd, 1)
+    eng = _bits(topo.mask(core, a) & topo.mask(core, ab) & topo.mask(core, b))
+    half = len(eng) // 2
+    sent = 0
+    trs = []
+    for j, blk in enumerate(pair):
+        w = int(T.cores[blk])
+        m = sum(eng[j * half:(j + 1) * half])
+        near = (w == a)
+        trs.append(RemoteDMATransfer(dst_ids=[_dst(topo, w, core)], dma_engine_mask=m,
+                                     remote_sem=S.in_ka if near else S.in_kb,
+                                     src=_blk(T.tx, j), dst=_blk(T.rx, 3 if near else 4)))
+        sent += _n(m)
+    g.remote_dma_fused(trs, local_sem=S.sent)
+    m = sum(eng)
+    g.wait_ge(S.k_n, n_own + _n(topo.mask(P[u]["c"], core)))
+    g.remote_dma_fused([RemoteDMATransfer(
+        dst_ids=[_dst(topo, b, core), _dst(topo, a, core), _dst(topo, ab, core)], dma_engine_mask=m, remote_sem=S.in_n,
+        srcs=[T.nb[:, 0:2]], dsts=[T.nb[:, 1:3], T.nb[:, 3:5], T.nb[:, 5:7]])], local_sem=S.sent)
+    sent += _n(m)
+    g.wait_ge(S.sent, sent)
+
+
+def _rank(g, t, T, topo, P):
+    rk = T.rank_of
+    S = T.sem
+    A = AluOpType
+    a, b, c, d, k = P[t]["a"], P[t]["b"], P[t]["c"], P[t]["d"], P[t]["k"]
+    kc = P[c]["k"]
+    bound = float(T.tables["BOUND"])
+    groups = [sorted([rk(P[c]["a"]), rk(P[d]["a"])]),
+              sorted([rk(a), rk(P[b]["a"])]),
+              sorted([rk(b), rk(d)]),
+              sorted([rk(t), rk(c)])]
+    slot = {}
+    for i, grp in enumerate(groups):
+        for j, blk in enumerate(grp):
+            slot[blk] = 2 * i + j
+
+    lds = [S.ld1, S.ld2, S.ld3, S.ld4]
+    ldn = []
+    for i, grp in enumerate(groups):
+        q = g.sync if i % 2 == 0 else g.scalar
+        if grp[1] == grp[0] + 1:
+            q.dma_start(_blk(T.gb, 2 * i, 2), _blk(T.gr, grp[0], 2)).then_inc(lds[i], 16)
+            ldn.append(16)
+        else:
+            for j, blk in enumerate(grp):
+                q.dma_start(_blk(T.gb, 2 * i + j), _blk(T.gr, blk)).then_inc(lds[i], 16)
+            ldn.append(32)
+
+    off = topo.mask(t, kc) & topo.mask(t, b) & topo.mask(t, c)
+    ob = _bits(off)
+    m_cab, m_sw = sum(ob[1::2]), sum(ob[0::2])
+    m_on = topo.mask(t, k) & ~off
+    sent = 0
+
+    def send(dst, out_ap, in_ap, sem, m):
+        rid, pid = topo.addr(dst, t)
+        g.remote_dma(out_ap=out_ap, in_ap=in_ap, remote_sem=sem, local_sem=S.sent, pid=pid, routing_id=rid,
+                     dma_engine_mask=m)
+        return _n(m)
+
+    g.wait_ge(S.ld1, ldn[0])
+    sent += send(kc, _blk(T.gb, 2, 2), _blk(T.gb, 0, 2), S.k_in, m_cab)
+    g.wait_ge(S.ld2, ldn[1])
+    sent += send(k, _blk(T.gb, 0, 2), _blk(T.gb, 2, 2), S.k_in, m_on)
+    g.wait_ge(S.ld3, ldn[2])
+    sent += send(b, _blk(T.rx, 0, 2), _blk(T.gb, 4, 2), S.in_b, m_sw)
+
+    v = g.vector
+    cst, sc = T.sm[:, 16:23], T.sm[:, 8:15]
+    v.memset(T.sm[:, 16:22], 0.0).then_inc(S.vc, 1)
+    v.memset(T.sm[:, 22:23], 1.0).then_inc(S.vc, 1)
+    pos = {blk: j for j, blk in enumerate(sorted([rk(t), rk(c)]))}
+    v.wait_ge(S.ld4, ldn[3])
+    v.wait_ge(S.in_b, _n(m_sw))
+    v.tensor_tensor(_blk(T.tx, 0), _blk(T.gb, slot[rk(c)]), _blk(T.rx, pos[rk(c)]), A.add).then_inc(S.vd, 1)
+    v.tensor_tensor(T.acc[:, :], _blk(T.gb, slot[rk(t)]), _blk(T.rx, pos[rk(t)]), A.add).then_inc(S.va, 1)
+
+    g.wait_ge(S.vd, 1)
+    sent += send(c, _blk(T.rx, 2), _blk(T.tx, 0), S.in_c, off)
+
+    nk = _n(off) // 2
+    for i, (sem, cnt, j) in enumerate([(S.in_c, _n(off), 2), (S.in_ka, nk, 3), (S.in_kb, nk, 4)]):
+        v.wait_ge(sem, cnt)
+        v.wait_ge(S.va, i + 1)
+        v.tensor_tensor(T.acc[:, :], T.acc[:, :], _blk(T.rx, j), A.add).then_inc(S.va, 1)
+
+    ss = T.sm[:, 0:1]
+    g.scalar.wait_ge(S.va, 4)
+    g.scalar.activation(T.yo[:, :], T.acc[:, :], ActivationFunctionType.Square, scale=1.0 / bound,
+                        accum_out=ss).then_inc(S.sq, 1)
+
+    g.wait_ge(S.sq, 1)
+    g.remote_dma_fused([
+        RemoteDMATransfer(dst_ids=[_dst(topo, kc, t)], dma_engine_mask=off, remote_sem=S.k_n, src=ss, dst=T.nb[:, 1:2]),
+        RemoteDMATransfer(dst_ids=[_dst(topo, k, t)], dma_engine_mask=m_on, remote_sem=S.k_n, src=ss, dst=T.nb[:, 0:1]),
+    ], local_sem=S.sent)
+    sent += _n(off) + _n(m_on)
+    sent += send(c, T.nb[:, 0:1], ss, S.in_n, off)
+
+    x, q, rx_, tt, t2, vv = T.sm[:, 14:15], T.sm[:, 4:5], T.sm[:, 5:6], T.sm[:, 6:7], T.sm[:, 7:8], T.sm[:, 23:24]
+    v.wait_ge(S.sq, 1)
+    v.wait_ge(S.vc, 2)
+    v.wait_ge(S.in_n, 4 * _n(off))
+    v.tensor_tensor_scan(sc, T.nb[:, 0:7], cst, ss, A.add, A.max).then_inc(S.vx, 1)
+    g.scalar.wait_ge(S.vx, 1)
+    g.scalar.activation(q, x, ActivationFunctionType.Sqrt, scale=2.0 ** -48).then_inc(S.sr, 1)
+    v.wait_ge(S.vx, 1)
+    v.reciprocal(rx_, x).then_inc(S.vx, 1)
+    g.scalar.wait_ge(S.vx, 2)
+    g.scalar.wait_ge(S.sr, 1)
+    g.scalar.activation(vv, q, ActivationFunctionType.Copy, scale=rx_).then_inc(S.sr, 1)
+    v.wait_ge(S.vx, 2)
+    v.wait_ge(S.sr, 1)
+    v.tensor_scalar(tt, q, q, rx_, A.mult, A.mult).then_inc(S.vx, 1)
+    v.wait_ge(S.vx, 3)
+    v.tensor_scalar(t2, tt, -(2.0 ** 71), 1.5 * 2.0 ** 24, A.mult, A.add).then_inc(S.vx, 1)
+    v.wait_ge(S.vx, 4)
+    v.wait_ge(S.sr, 2)
+    v.tensor_scalar(T.yo[:, :], T.acc[:, :], t2, vv, A.mult, A.mult).then_inc(S.vy, 1)
+
+    g.sync.wait_ge(S.vy, 1)
+    g.sync.dma_start(T.y[:, :], T.yo[:, :]).then_inc(S.st, 16)
+    g.wait_ge(S.sent, sent)
+    g.wait_ge(S.st, 16)
+
+
+def rank_program(g, core, T, topo):
+    P = _plan(T, topo)
+    if core in P:
+        _rank(g, core, T, topo, P)
+        return
+    for u in P:
+        if P[u]["k"] == core:
+            _helper(g, core, u, T, topo, P)
+            return

@@ -5,16 +5,17 @@ F = 128
 SIM_CORES = 512
 
 SCRATCH = {
-    "gb": ("sbuf", [128, 8 * F], "float32"),
-    "rx": ("sbuf", [128, 5 * F], "float32"),
-    "tx": ("sbuf", [128, 2 * F], "float32"),
+    "dx": ("dram", [6, 128, F], "float32"),
+    "dr": ("dram", [128, F], "float32"),
+    "gb": ("sbuf", [128, 2 * F], "float32"),
+    "rx": ("sbuf", [128, 6 * F], "float32"),
     "nb": ("sbuf", [128, 8], "float32"),
     "sm": ("sbuf", [128, 24], "float32"),
     "yo": ("sbuf", [128, F], "float32"),
     "acc": ("psum", [128, F], "float32"),
 }
-SEMAPHORES = ["ld1", "ld2", "ld3", "ld4", "sent", "in_b", "in_c", "in_ka", "in_kb", "in_n", "k_in", "k_n",
-              "vc", "vd", "va", "sq", "vx", "sr", "vy", "st"]
+SEMAPHORES = ["ld1", "ld2", "ld3", "ld4", "ld5", "go", "sent", "in_b", "in_bb", "in_c", "in_e1", "in_e2", "in_l1", "in_l2",
+              "in_n", "in_nb", "k_own", "k_cab", "k_n", "vc", "va", "sq", "vx", "sr", "vy", "st"]
 
 _PLAN = {}
 
@@ -31,7 +32,7 @@ def _plan(T, topo):
         a = [u for u in ranks if u != t and topo.host(u) == topo.host(t)][0]
         k = [x for x in range(SIM_CORES)
              if x != t and topo.host(x) == topo.host(t) and topo.chip(x) == topo.chip(t)
-             and topo.die(x) == topo.die(t) and topo.may_write(x, a)][0]
+             and topo.die(x) == topo.die(t) and topo.may_write(x, a)][:2]
         _PLAN[t] = {"a": a, "b": b, "c": c, "d": d, "k": k}
     return _PLAN
 
@@ -44,6 +45,16 @@ def _n(m):
     return len(_bits(m))
 
 
+def _masks(topo, t, P):
+    b, c = P[t]["b"], P[t]["c"]
+    off = topo.mask(t, P[c]["k"][0]) & topo.mask(t, P[c]["k"][1]) & topo.mask(t, b) & topo.mask(t, c)
+    ob = _bits(off)
+    cab, sw = ob[1::2], ob[0::2]
+    on = _bits(topo.mask(t, P[t]["k"][0]) & topo.mask(t, P[t]["k"][1]) & ~off)
+    h = len(on) // 2
+    return {"off": off, "sw": sum(sw), "cab": sum(cab), "on": [sum(on[:h]), sum(on[h:])], "on_all": sum(on)}
+
+
 def _dst(topo, dst, src):
     rid, pid = topo.addr(dst, src)
     return DstId(rid=rid, pnc=pid)
@@ -53,36 +64,30 @@ def _blk(buf, j, n=1):
     return buf[:, j * F:(j + n) * F]
 
 
-def _helper(g, core, u, T, topo, P):
-    rk = T.rank_of
+def _helper(g, core, u, i, T, topo, P):
     S = T.sem
-    a, b = P[u]["a"], P[u]["b"]
-    ab = P[b]["a"]
-    pair = sorted([rk(a), rk(ab)])
-    n_own = _n(topo.mask(u, core) & ~topo.mask(u, P[u]["c"]))
-    n_cab = _n(topo.mask(P[u]["c"], core)) // 2
-    g.vector.wait_ge(S.k_in, n_own + n_cab)
-    g.vector.tensor_tensor(T.tx[:, 0:2 * F], T.gb[:, 0:2 * F], T.gb[:, 2 * F:4 * F], AluOpType.add).then_inc(S.vd, 1)
-    g.wait_ge(S.vd, 1)
-    eng = _bits(topo.mask(core, a) & topo.mask(core, ab) & topo.mask(core, b))
-    half = len(eng) // 2
+    a, b, c = P[u]["a"], P[u]["b"], P[u]["c"]
+    ab, ac = P[b]["a"], P[c]["a"]
+    Mu, Mc = _masks(topo, u, P), _masks(topo, c, P)
+    if i == 0:
+        jobs = [(ac, _n(Mu["on"][0]), S.in_e1, 2), (a, _n(Mu["on_all"]), S.in_l1, 4)]
+    else:
+        jobs = [(ab, _n(Mu["on"][1]), S.in_e2, 3), (ab, _n(Mc["cab"]), S.in_l2, 5)]
     sent = 0
-    trs = []
-    for j, blk in enumerate(pair):
-        w = int(T.cores[blk])
-        m = sum(eng[j * half:(j + 1) * half])
-        near = (w == a)
-        trs.append(RemoteDMATransfer(dst_ids=[_dst(topo, w, core)], dma_engine_mask=m,
-                                     remote_sem=S.in_ka if near else S.in_kb,
-                                     src=_blk(T.tx, j), dst=_blk(T.rx, 3 if near else 4)))
+    for j, (w, cnt, sem, sl) in enumerate(jobs):
+        m = topo.mask(core, w)
+        rid, pid = topo.addr(w, core)
+        g.wait_ge(S.k_own if j == 0 else S.k_cab, cnt)
+        g.remote_dma(out_ap=_blk(T.rx, sl), in_ap=T.dx[j], remote_sem=sem, local_sem=S.sent,
+                     pid=pid, routing_id=rid, dma_engine_mask=m)
         sent += _n(m)
-    g.remote_dma_fused(trs, local_sem=S.sent)
-    m = sum(eng)
-    g.wait_ge(S.k_n, n_own + _n(topo.mask(P[u]["c"], core)))
-    g.remote_dma_fused([RemoteDMATransfer(
-        dst_ids=[_dst(topo, b, core), _dst(topo, a, core), _dst(topo, ab, core)], dma_engine_mask=m, remote_sem=S.in_n,
-        srcs=[T.nb[:, 0:2]], dsts=[T.nb[:, 1:3], T.nb[:, 3:5], T.nb[:, 5:7]])], local_sem=S.sent)
-    sent += _n(m)
+    if i == 0:
+        m4 = topo.mask(core, a) & topo.mask(core, ab)
+        g.wait_ge(S.k_n, _n(Mu["on_all"]) + _n(Mc["off"]))
+        g.remote_dma_fused([RemoteDMATransfer(
+            dst_ids=[_dst(topo, a, core), _dst(topo, ab, core)], dma_engine_mask=m4,
+            remote_sem=S.in_n, srcs=[T.nb[:, 0:2]], dsts=[T.nb[:, 3:5], T.nb[:, 5:7]])], local_sem=S.sent)
+        sent += _n(m4)
     g.wait_ge(S.sent, sent)
 
 
@@ -90,34 +95,30 @@ def _rank(g, t, T, topo, P):
     rk = T.rank_of
     S = T.sem
     A = AluOpType
-    a, b, c, d, k = P[t]["a"], P[t]["b"], P[t]["c"], P[t]["d"], P[t]["k"]
-    kc = P[c]["k"]
+    a, b, c, d = P[t]["a"], P[t]["b"], P[t]["c"], P[t]["d"]
+    k, kc = P[t]["k"], P[c]["k"]
     bound = float(T.tables["BOUND"])
-    groups = [sorted([rk(P[c]["a"]), rk(P[d]["a"])]),
-              sorted([rk(a), rk(P[b]["a"])]),
-              sorted([rk(b), rk(d)]),
-              sorted([rk(t), rk(c)])]
-    slot = {}
-    for i, grp in enumerate(groups):
-        for j, blk in enumerate(grp):
-            slot[blk] = 2 * i + j
+    M = _masks(topo, t, P)
+    off = M["off"]
 
-    lds = [S.ld1, S.ld2, S.ld3, S.ld4]
-    ldn = []
-    for i, grp in enumerate(groups):
-        q = g.sync if i % 2 == 0 else g.scalar
-        if grp[1] == grp[0] + 1:
-            q.dma_start(_blk(T.gb, 2 * i, 2), _blk(T.gr, grp[0], 2)).then_inc(lds[i], 16)
-            ldn.append(16)
-        else:
-            for j, blk in enumerate(grp):
-                q.dma_start(_blk(T.gb, 2 * i + j), _blk(T.gr, blk)).then_inc(lds[i], 16)
-            ldn.append(32)
+    g.sync.dma_start(T.dx[1], _blk(T.gr, rk(P[b]["a"]))).then_inc(S.ld1, 16)
+    g.scalar.dma_start(T.dx[2], _blk(T.gr, rk(P[c]["a"]))).then_inc(S.ld1, 16)
+    g.sync.dma_start(T.dx[3], _blk(T.gr, rk(P[d]["a"]))).then_inc(S.ld2, 16)
+    g.scalar.dma_start(T.dx[4], _blk(T.gr, rk(d))).then_inc(S.ld2, 16)
+    g.scalar.dma_start(T.dx[5], _blk(T.gr, rk(c))).then_inc(S.ld4, 16)
+    g.sync.wait_ge(S.go, 1)
+    g.sync.dma_start(T.dx[0], _blk(T.gr, rk(a))).then_inc(S.ld5, 16)
+    pair = sorted([rk(t), rk(b)])
+    slot = {blk: j for j, blk in enumerate(pair)}
+    g.scalar.wait_ge(S.go, 1)
+    if pair[1] == pair[0] + 1:
+        g.scalar.dma_start(_blk(T.gb, 0, 2), _blk(T.gr, pair[0], 2)).then_inc(S.ld3, 16)
+        ld3 = 16
+    else:
+        for j, blk in enumerate(pair):
+            g.scalar.dma_start(_blk(T.gb, j), _blk(T.gr, blk)).then_inc(S.ld3, 16)
+        ld3 = 32
 
-    off = topo.mask(t, kc) & topo.mask(t, b) & topo.mask(t, c)
-    ob = _bits(off)
-    m_cab, m_sw = sum(ob[1::2]), sum(ob[0::2])
-    m_on = topo.mask(t, k) & ~off
     sent = 0
 
     def send(dst, out_ap, in_ap, sem, m):
@@ -126,48 +127,75 @@ def _rank(g, t, T, topo, P):
                      dma_engine_mask=m)
         return _n(m)
 
-    g.wait_ge(S.ld1, ldn[0])
-    sent += send(kc, _blk(T.gb, 2, 2), _blk(T.gb, 0, 2), S.k_in, m_cab)
-    g.wait_ge(S.ld2, ldn[1])
-    sent += send(k, _blk(T.gb, 0, 2), _blk(T.gb, 2, 2), S.k_in, m_on)
-    g.wait_ge(S.ld3, ldn[2])
-    sent += send(b, _blk(T.rx, 0, 2), _blk(T.gb, 4, 2), S.in_b, m_sw)
+    g.wait_ge(S.ld1, 32)
+    g.remote_dma_fused([
+        RemoteDMATransfer(dst_ids=[_dst(topo, k[0], t)], dma_engine_mask=M["on"][0], remote_sem=S.k_own,
+                          src=T.dx[2], dst=T.dx[0]),
+        RemoteDMATransfer(dst_ids=[_dst(topo, k[1], t)], dma_engine_mask=M["on"][1], remote_sem=S.k_own,
+                          src=T.dx[1], dst=T.dx[0]),
+    ], local_sem=S.sent)
+    sent += _n(M["on_all"])
+    g.wait_ge(S.ld2, 32)
+    g.remote_dma_fused([
+        RemoteDMATransfer(dst_ids=[_dst(topo, kc[1], t)], dma_engine_mask=M["cab"], remote_sem=S.k_cab,
+                          src=T.dx[3], dst=T.dx[1]),
+        RemoteDMATransfer(dst_ids=[_dst(topo, b, t)], dma_engine_mask=M["sw"], remote_sem=S.in_b,
+                          src=T.dx[4], dst=T.dr[:, :]),
+    ], local_sem=S.sent)
+    sent += _n(off)
+    g.sem_inc(S.go, 1)
+    g.wait_ge(S.ld5, 16)
+    g.wait_ge(S.ld3, ld3)
+    g.remote_dma_fused([
+        RemoteDMATransfer(dst_ids=[_dst(topo, k[0], t)], dma_engine_mask=M["on_all"], remote_sem=S.k_cab,
+                          src=T.dx[0], dst=T.dx[1]),
+        RemoteDMATransfer(dst_ids=[_dst(topo, b, t)], dma_engine_mask=off, remote_sem=S.in_bb,
+                          src=_blk(T.gb, slot[rk(b)]), dst=_blk(T.rx, 0)),
+    ], local_sem=S.sent)
+    sent += _n(M["on_all"]) + _n(off)
+
+    g.wait_ge(S.ld4, 16)
+    g.wait_ge(S.in_b, _n(M["sw"]))
+    g.remote_dma_fused([RemoteDMATransfer(dst_ids=[_dst(topo, c, t)], dma_engine_mask=off, remote_sem=S.in_c,
+                                          srcs=[T.dx[5], T.dr[:, :]], dsts=[_blk(T.rx, 1)], alu_op=1)], local_sem=S.sent)
+    sent += _n(off)
 
     v = g.vector
     cst, sc = T.sm[:, 16:23], T.sm[:, 8:15]
     v.memset(T.sm[:, 16:22], 0.0).then_inc(S.vc, 1)
     v.memset(T.sm[:, 22:23], 1.0).then_inc(S.vc, 1)
-    pos = {blk: j for j, blk in enumerate(sorted([rk(t), rk(c)]))}
-    v.wait_ge(S.ld4, ldn[3])
-    v.wait_ge(S.in_b, _n(m_sw))
-    v.tensor_tensor(_blk(T.tx, 0), _blk(T.gb, slot[rk(c)]), _blk(T.rx, pos[rk(c)]), A.add).then_inc(S.vd, 1)
-    v.tensor_tensor(T.acc[:, :], _blk(T.gb, slot[rk(t)]), _blk(T.rx, pos[rk(t)]), A.add).then_inc(S.va, 1)
-
-    g.wait_ge(S.vd, 1)
-    sent += send(c, _blk(T.rx, 2), _blk(T.tx, 0), S.in_c, off)
-
-    nk = _n(off) // 2
-    for i, (sem, cnt, j) in enumerate([(S.in_c, _n(off), 2), (S.in_ka, nk, 3), (S.in_kb, nk, 4)]):
-        v.wait_ge(sem, cnt)
-        v.wait_ge(S.va, i + 1)
-        v.tensor_tensor(T.acc[:, :], T.acc[:, :], _blk(T.rx, j), A.add).then_inc(S.va, 1)
+    ne = _n(off)
+    parts = [(S.in_e1, 2), (S.in_e2, 3), (S.in_bb, 0), (S.in_l1, 4), (S.in_l2, 5), (S.in_c, 1)]
+    v.wait_ge(S.ld3, ld3)
+    for i, (sem, j) in enumerate(parts):
+        v.wait_ge(sem, ne)
+        if i == 0:
+            v.tensor_tensor(T.acc[:, :], _blk(T.gb, slot[rk(t)]), _blk(T.rx, j), A.add).then_inc(S.va, 1)
+        else:
+            v.wait_ge(S.va, i)
+            v.tensor_tensor(T.acc[:, :], T.acc[:, :], _blk(T.rx, j), A.add).then_inc(S.va, 1)
 
     ss = T.sm[:, 0:1]
-    g.scalar.wait_ge(S.va, 4)
+    g.scalar.wait_ge(S.va, len(parts))
     g.scalar.activation(T.yo[:, :], T.acc[:, :], ActivationFunctionType.Square, scale=1.0 / bound,
                         accum_out=ss).then_inc(S.sq, 1)
 
     g.wait_ge(S.sq, 1)
     g.remote_dma_fused([
-        RemoteDMATransfer(dst_ids=[_dst(topo, kc, t)], dma_engine_mask=off, remote_sem=S.k_n, src=ss, dst=T.nb[:, 1:2]),
-        RemoteDMATransfer(dst_ids=[_dst(topo, k, t)], dma_engine_mask=m_on, remote_sem=S.k_n, src=ss, dst=T.nb[:, 0:1]),
+        RemoteDMATransfer(dst_ids=[_dst(topo, kc[0], t)], dma_engine_mask=off, remote_sem=S.k_n, src=ss, dst=T.nb[:, 1:2]),
+        RemoteDMATransfer(dst_ids=[_dst(topo, k[0], t)], dma_engine_mask=M["on_all"], remote_sem=S.k_n, src=ss,
+                          dst=T.nb[:, 0:1]),
     ], local_sem=S.sent)
-    sent += _n(off) + _n(m_on)
+    sent += _n(off) + _n(M["on_all"])
+    sent += send(b, T.nb[:, 1:2], ss, S.in_nb, off)
     sent += send(c, T.nb[:, 0:1], ss, S.in_n, off)
+    g.wait_ge(S.in_nb, _n(off))
+    sent += send(c, T.nb[:, 2:3], T.nb[:, 1:2], S.in_n, off)
 
     x, q, rx_, tt, t2, vv = T.sm[:, 14:15], T.sm[:, 4:5], T.sm[:, 5:6], T.sm[:, 6:7], T.sm[:, 7:8], T.sm[:, 23:24]
     v.wait_ge(S.sq, 1)
     v.wait_ge(S.vc, 2)
+    v.wait_ge(S.in_nb, _n(off))
     v.wait_ge(S.in_n, 4 * _n(off))
     v.tensor_tensor_scan(sc, T.nb[:, 0:7], cst, ss, A.add, A.max).then_inc(S.vx, 1)
     g.scalar.wait_ge(S.vx, 1)
@@ -198,6 +226,7 @@ def rank_program(g, core, T, topo):
         _rank(g, core, T, topo, P)
         return
     for u in P:
-        if P[u]["k"] == core:
-            _helper(g, core, u, T, topo, P)
-            return
+        for i, x in enumerate(P[u]["k"]):
+            if x == core:
+                _helper(g, core, u, i, T, topo, P)
+                return

@@ -3,19 +3,33 @@ from concourse.mybir import AluOpType, ActivationFunctionType
 
 F = 128
 SIM_CORES = 512
+NT = 63
+POLY = [0.6324555277824402, -0.12649111449718475, 0.037947334349155426, -0.012649068608880043, 0.004427172243595123,
+        -0.0015941152814775705, 0.000584517081733793, -0.00021592207485809922, 8.095185330603272e-05,
+        -3.286140781710856e-05, 1.2511882232502103e-05, -2.1995615497871768e-06, 8.244879268204386e-07,
+        -2.078896613966208e-06, 8.101333719423565e-07, 4.023792712359864e-07, -1.5789640883667744e-07,
+        -9.76745511138688e-08, 3.818073324168836e-08]
+W = len(POLY) - 1
+L = NT + W
 
 SCRATCH = {
     "dx": ("dram", [6, 128, F], "float32"),
     "dr": ("dram", [128, F], "float32"),
     "gb": ("sbuf", [128, 2 * F], "float32"),
     "rx": ("sbuf", [128, 6 * F], "float32"),
-    "nb": ("sbuf", [128, 8], "float32"),
+    "nb": ("sbuf", [128, 12], "float32"),
     "sm": ("sbuf", [128, 24], "float32"),
+    "ta": ("sbuf", [128, NT + 1], "float32"),
+    "hb": ("sbuf", [128, L + 3], "float32"),
+    "d1": ("sbuf", [128, L + 3], "float32"),
+    "ob": ("sbuf", [128, L + NT + 4], "float32"),
+    "cf": ("sbuf", [128, L + 3], "float32"),
+    "rb": ("sbuf", [128, L + 3], "float32"),
     "yo": ("sbuf", [128, F], "float32"),
     "acc": ("psum", [128, F], "float32"),
 }
 SEMAPHORES = ["ld1", "ld2", "ld3", "ld4", "ld5", "go", "sent", "in_b", "in_bb", "in_c", "in_e1", "in_e2", "in_l1", "in_l2",
-              "in_n", "in_nb", "k_own", "k_cab", "k_n", "vc", "va", "sq", "vx", "sr", "vy", "st"]
+              "in_n", "in_nb", "k_own", "k_cab", "k_n", "vc", "va", "sq", "vx", "vy", "st"]
 
 _PLAN = {}
 
@@ -86,7 +100,7 @@ def _helper(g, core, u, i, T, topo, P):
         g.wait_ge(S.k_n, _n(Mu["on_all"]) + _n(Mc["off"]))
         g.remote_dma_fused([RemoteDMATransfer(
             dst_ids=[_dst(topo, a, core), _dst(topo, ab, core)], dma_engine_mask=m4,
-            remote_sem=S.in_n, srcs=[T.nb[:, 0:2]], dsts=[T.nb[:, 3:5], T.nb[:, 5:7]])], local_sem=S.sent)
+            remote_sem=S.in_n, srcs=[T.nb[:, 0:2]], dsts=[T.nb[:, 7:9], T.nb[:, 9:11]])], local_sem=S.sent)
         sent += _n(m4)
     g.wait_ge(S.sent, sent)
 
@@ -162,8 +176,17 @@ def _rank(g, t, T, topo, P):
 
     v = g.vector
     cst, sc = T.sm[:, 16:23], T.sm[:, 8:15]
-    v.memset(T.sm[:, 16:22], 0.0).then_inc(S.vc, 1)
-    v.memset(T.sm[:, 22:23], 1.0).then_inc(S.vc, 1)
+    fills = [(T.sm[:, 16:22], 0.0), (T.sm[:, 22:23], 1.0),
+             (T.d1[:, 0:NT], 0.0), (T.d1[:, NT:NT + 1], -2.5), (T.d1[:, NT + 1:L], 0.0),
+             (T.hb[:, 0:NT], 4.0), (T.hb[:, NT:L], 1.0), (T.cf[:, W:L], 0.0)]
+    fills += [(T.cf[:, j:j + 1], float(POLY[W - 1 - j])) for j in range(W)]
+    for ap, val in fills:
+        v.memset(ap, val).then_inc(S.vc, 1)
+    nc = len(fills)
+    v.wait_ge(S.vc, nc)
+    v.tensor_tensor_scan(T.ta[:, 0:NT], T.hb[:, 0:NT], T.d1[:, 0:NT], 1.0, A.mult, A.add).then_inc(S.vc, 1)
+    nc += 1
+
     ne = _n(off)
     parts = [(S.in_e1, 2), (S.in_e2, 3), (S.in_bb, 0), (S.in_l1, 4), (S.in_l2, 5), (S.in_c, 1)]
     v.wait_ge(S.ld3, ld3)
@@ -175,7 +198,7 @@ def _rank(g, t, T, topo, P):
             v.wait_ge(S.va, i)
             v.tensor_tensor(T.acc[:, :], T.acc[:, :], _blk(T.rx, j), A.add).then_inc(S.va, 1)
 
-    ss = T.sm[:, 0:1]
+    ss = T.nb[:, 3:4]
     g.scalar.wait_ge(S.va, len(parts))
     g.scalar.activation(T.yo[:, :], T.acc[:, :], ActivationFunctionType.Square, scale=1.0 / bound,
                         accum_out=ss).then_inc(S.sq, 1)
@@ -187,32 +210,25 @@ def _rank(g, t, T, topo, P):
                           dst=T.nb[:, 0:1]),
     ], local_sem=S.sent)
     sent += _n(off) + _n(M["on_all"])
-    sent += send(b, T.nb[:, 1:2], ss, S.in_nb, off)
-    sent += send(c, T.nb[:, 0:1], ss, S.in_n, off)
+    sent += send(b, T.nb[:, 4:5], ss, S.in_nb, off)
     g.wait_ge(S.in_nb, _n(off))
-    sent += send(c, T.nb[:, 2:3], T.nb[:, 1:2], S.in_n, off)
+    sent += send(c, T.nb[:, 5:7], T.nb[:, 3:5], S.in_n, off)
 
-    x, q, rx_, tt, t2, vv = T.sm[:, 14:15], T.sm[:, 4:5], T.sm[:, 5:6], T.sm[:, 6:7], T.sm[:, 7:8], T.sm[:, 23:24]
+    x = T.sm[:, 14:15]
     v.wait_ge(S.sq, 1)
-    v.wait_ge(S.vc, 2)
+    v.wait_ge(S.vc, nc)
     v.wait_ge(S.in_nb, _n(off))
-    v.wait_ge(S.in_n, 4 * _n(off))
-    v.tensor_tensor_scan(sc, T.nb[:, 0:7], cst, ss, A.add, A.max).then_inc(S.vx, 1)
-    g.scalar.wait_ge(S.vx, 1)
-    g.scalar.activation(q, x, ActivationFunctionType.Sqrt, scale=2.0 ** -48).then_inc(S.sr, 1)
+    v.wait_ge(S.in_n, 3 * _n(off))
+    v.tensor_tensor_scan(sc, T.nb[:, 4:11], cst, ss, A.add, A.max).then_inc(S.vx, 1)
     v.wait_ge(S.vx, 1)
-    v.reciprocal(rx_, x).then_inc(S.vx, 1)
-    g.scalar.wait_ge(S.vx, 2)
-    g.scalar.wait_ge(S.sr, 1)
-    g.scalar.activation(vv, q, ActivationFunctionType.Copy, scale=rx_).then_inc(S.sr, 1)
+    v.tensor_scalar(T.hb[:, 0:NT], T.ta[:, 0:NT], x, 0.25, A.is_gt, A.max).then_inc(S.vx, 1)
     v.wait_ge(S.vx, 2)
-    v.wait_ge(S.sr, 1)
-    v.tensor_scalar(tt, q, q, rx_, A.mult, A.mult).then_inc(S.vx, 1)
-    v.wait_ge(S.vx, 3)
-    v.tensor_scalar(t2, tt, -(2.0 ** 71), 1.5 * 2.0 ** 24, A.mult, A.add).then_inc(S.vx, 1)
+    v.tensor_tensor_scan(T.ob[:, 0:L], T.hb[:, 0:L], T.d1[:, 0:L], x, A.mult, A.add).then_inc(S.vx, 1)
+    v.tensor_scalar(T.ob[:, L:L + NT], T.hb[:, 0:NT], 0.5, None, A.max).then_inc(S.vx, 1)
     v.wait_ge(S.vx, 4)
-    v.wait_ge(S.sr, 2)
-    v.tensor_scalar(T.yo[:, :], T.acc[:, :], t2, vv, A.mult, A.mult).then_inc(S.vy, 1)
+    v.tensor_tensor_scan(T.rb[:, 0:L], T.ob[:, NT:NT + L], T.cf[:, 0:L], float(POLY[W]), A.mult, A.add).then_inc(S.vx, 1)
+    v.wait_ge(S.vx, 5)
+    v.tensor_scalar(T.yo[:, :], T.acc[:, :], T.rb[:, L - 1:L], None, A.mult).then_inc(S.vy, 1)
 
     g.sync.wait_ge(S.vy, 1)
     g.sync.dma_start(T.y[:, :], T.yo[:, :]).then_inc(S.st, 16)

from concourse.bass import DstId, RemoteDMATransfer
from concourse.mybir import AluOpType, ActivationFunctionType

F = 128
SIM_CORES = 512
NT = 63
POLY = [0.6324555277824402, -0.12649111449718475, 0.037947334349155426, -0.012649068608880043, 0.004427172243595123,
        -0.0015941152814775705, 0.000584517081733793, -0.00021592207485809922, 8.095185330603272e-05,
        -3.286140781710856e-05, 1.2511882232502103e-05, -2.1995615497871768e-06, 8.244879268204386e-07,
        -2.078896613966208e-06, 8.101333719423565e-07, 4.023792712359864e-07, -1.5789640883667744e-07,
        -9.76745511138688e-08, 3.818073324168836e-08]
W = len(POLY) - 1
L = NT + W

SCRATCH = {
    "dx": ("dram", [6, 128, F], "float32"),
    "dr": ("dram", [128, F], "float32"),
    "gb": ("sbuf", [128, 2 * F], "float32"),
    "rx": ("sbuf", [128, 6 * F], "float32"),
    "nb": ("sbuf", [128, 12], "float32"),
    "sm": ("sbuf", [128, 24], "float32"),
    "ta": ("sbuf", [128, NT + 1], "float32"),
    "hb": ("sbuf", [128, L + 3], "float32"),
    "d1": ("sbuf", [128, L + 3], "float32"),
    "ob": ("sbuf", [128, L + NT + 4], "float32"),
    "cf": ("sbuf", [128, L + 3], "float32"),
    "rb": ("sbuf", [128, L + 3], "float32"),
    "yo": ("sbuf", [128, F], "float32"),
    "acc": ("psum", [128, F], "float32"),
}
SEMAPHORES = ["ld1", "ld2", "ld3", "ld4", "ld5", "go", "sent", "in_b", "in_bb", "in_c", "in_e1", "in_e2", "in_l1", "in_l2",
              "in_n", "in_nb", "k_own", "k_cab", "k_n", "vc", "va", "sq", "vx", "vy", "st"]

_PLAN = {}


def _plan(T, topo):
    if _PLAN:
        return _PLAN
    ranks = [int(u) for u in T.cores]
    for t in ranks:
        col = [u for u in ranks if u != t and topo.chip(u) == topo.chip(t)]
        b = [u for u in col if topo.same_plane(t, u)][0]
        c = [u for u in col if topo.may_write(t, u) and not topo.same_plane(t, u)][0]
        d = [u for u in col if not topo.may_write(t, u)][0]
        a = [u for u in ranks if u != t and topo.host(u) == topo.host(t)][0]
        k = [x for x in range(SIM_CORES)
             if x != t and topo.host(x) == topo.host(t) and topo.chip(x) == topo.chip(t)
             and topo.die(x) == topo.die(t) and topo.may_write(x, a)][:2]
        _PLAN[t] = {"a": a, "b": b, "c": c, "d": d, "k": k}
    return _PLAN


def _bits(m):
    return [1 << i for i in range(m.bit_length()) if (m >> i) & 1]


def _n(m):
    return len(_bits(m))


def _masks(topo, t, P):
    b, c = P[t]["b"], P[t]["c"]
    off = topo.mask(t, P[c]["k"][0]) & topo.mask(t, P[c]["k"][1]) & topo.mask(t, b) & topo.mask(t, c)
    ob = _bits(off)
    cab, sw = ob[1::2], ob[0::2]
    on = _bits(topo.mask(t, P[t]["k"][0]) & topo.mask(t, P[t]["k"][1]) & ~off)
    h = len(on) // 2
    return {"off": off, "sw": sum(sw), "cab": sum(cab), "on": [sum(on[:h]), sum(on[h:])], "on_all": sum(on)}


def _dst(topo, dst, src):
    rid, pid = topo.addr(dst, src)
    return DstId(rid=rid, pnc=pid)


def _blk(buf, j, n=1):
    return buf[:, j * F:(j + n) * F]


def _helper(g, core, u, i, T, topo, P):
    S = T.sem
    a, b, c = P[u]["a"], P[u]["b"], P[u]["c"]
    ab, ac = P[b]["a"], P[c]["a"]
    Mu, Mc = _masks(topo, u, P), _masks(topo, c, P)
    if i == 0:
        jobs = [(ac, _n(Mu["on"][0]), S.in_e1, 2), (a, _n(Mu["on_all"]), S.in_l1, 4)]
    else:
        jobs = [(ab, _n(Mu["on"][1]), S.in_e2, 3), (ab, _n(Mc["cab"]), S.in_l2, 5)]
    sent = 0
    for j, (w, cnt, sem, sl) in enumerate(jobs):
        m = topo.mask(core, w)
        rid, pid = topo.addr(w, core)
        g.wait_ge(S.k_own if j == 0 else S.k_cab, cnt)
        g.remote_dma(out_ap=_blk(T.rx, sl), in_ap=T.dx[j], remote_sem=sem, local_sem=S.sent,
                     pid=pid, routing_id=rid, dma_engine_mask=m)
        sent += _n(m)
    if i == 0:
        m4 = topo.mask(core, a) & topo.mask(core, ab)
        g.wait_ge(S.k_n, _n(Mu["on_all"]) + _n(Mc["off"]))
        g.remote_dma_fused([RemoteDMATransfer(
            dst_ids=[_dst(topo, a, core), _dst(topo, ab, core)], dma_engine_mask=m4,
            remote_sem=S.in_n, srcs=[T.nb[:, 0:2]], dsts=[T.nb[:, 7:9], T.nb[:, 9:11]])], local_sem=S.sent)
        sent += _n(m4)
    g.wait_ge(S.sent, sent)


def _rank(g, t, T, topo, P):
    rk = T.rank_of
    S = T.sem
    A = AluOpType
    a, b, c, d = P[t]["a"], P[t]["b"], P[t]["c"], P[t]["d"]
    k, kc = P[t]["k"], P[c]["k"]
    bound = float(T.tables["BOUND"])
    M = _masks(topo, t, P)
    off = M["off"]

    g.sync.dma_start(T.dx[1], _blk(T.gr, rk(P[b]["a"]))).then_inc(S.ld1, 16)
    g.scalar.dma_start(T.dx[2], _blk(T.gr, rk(P[c]["a"]))).then_inc(S.ld1, 16)
    g.sync.dma_start(T.dx[3], _blk(T.gr, rk(P[d]["a"]))).then_inc(S.ld2, 16)
    g.scalar.dma_start(T.dx[4], _blk(T.gr, rk(d))).then_inc(S.ld2, 16)
    g.scalar.dma_start(T.dx[5], _blk(T.gr, rk(c))).then_inc(S.ld4, 16)
    g.sync.wait_ge(S.go, 1)
    g.sync.dma_start(T.dx[0], _blk(T.gr, rk(a))).then_inc(S.ld5, 16)
    pair = sorted([rk(t), rk(b)])
    slot = {blk: j for j, blk in enumerate(pair)}
    g.scalar.wait_ge(S.go, 1)
    if pair[1] == pair[0] + 1:
        g.scalar.dma_start(_blk(T.gb, 0, 2), _blk(T.gr, pair[0], 2)).then_inc(S.ld3, 16)
        ld3 = 16
    else:
        for j, blk in enumerate(pair):
            g.scalar.dma_start(_blk(T.gb, j), _blk(T.gr, blk)).then_inc(S.ld3, 16)
        ld3 = 32

    sent = 0

    def send(dst, out_ap, in_ap, sem, m):
        rid, pid = topo.addr(dst, t)
        g.remote_dma(out_ap=out_ap, in_ap=in_ap, remote_sem=sem, local_sem=S.sent, pid=pid, routing_id=rid,
                     dma_engine_mask=m)
        return _n(m)

    g.wait_ge(S.ld1, 32)
    g.remote_dma_fused([
        RemoteDMATransfer(dst_ids=[_dst(topo, k[0], t)], dma_engine_mask=M["on"][0], remote_sem=S.k_own,
                          src=T.dx[2], dst=T.dx[0]),
        RemoteDMATransfer(dst_ids=[_dst(topo, k[1], t)], dma_engine_mask=M["on"][1], remote_sem=S.k_own,
                          src=T.dx[1], dst=T.dx[0]),
    ], local_sem=S.sent)
    sent += _n(M["on_all"])
    g.wait_ge(S.ld2, 32)
    g.remote_dma_fused([
        RemoteDMATransfer(dst_ids=[_dst(topo, kc[1], t)], dma_engine_mask=M["cab"], remote_sem=S.k_cab,
                          src=T.dx[3], dst=T.dx[1]),
        RemoteDMATransfer(dst_ids=[_dst(topo, b, t)], dma_engine_mask=M["sw"], remote_sem=S.in_b,
                          src=T.dx[4], dst=T.dr[:, :]),
    ], local_sem=S.sent)
    sent += _n(off)
    g.sem_inc(S.go, 1)
    g.wait_ge(S.ld5, 16)
    g.wait_ge(S.ld3, ld3)
    g.remote_dma_fused([
        RemoteDMATransfer(dst_ids=[_dst(topo, k[0], t)], dma_engine_mask=M["on_all"], remote_sem=S.k_cab,
                          src=T.dx[0], dst=T.dx[1]),
        RemoteDMATransfer(dst_ids=[_dst(topo, b, t)], dma_engine_mask=off, remote_sem=S.in_bb,
                          src=_blk(T.gb, slot[rk(b)]), dst=_blk(T.rx, 0)),
    ], local_sem=S.sent)
    sent += _n(M["on_all"]) + _n(off)

    g.wait_ge(S.ld4, 16)
    g.wait_ge(S.in_b, _n(M["sw"]))
    g.remote_dma_fused([RemoteDMATransfer(dst_ids=[_dst(topo, c, t)], dma_engine_mask=off, remote_sem=S.in_c,
                                          srcs=[T.dx[5], T.dr[:, :]], dsts=[_blk(T.rx, 1)], alu_op=1)], local_sem=S.sent)
    sent += _n(off)

    v = g.vector
    cst, sc = T.sm[:, 16:23], T.sm[:, 8:15]
    fills = [(T.sm[:, 16:22], 0.0), (T.sm[:, 22:23], 1.0),
             (T.d1[:, 0:NT], 0.0), (T.d1[:, NT:NT + 1], -2.5), (T.d1[:, NT + 1:L], 0.0),
             (T.hb[:, 0:NT], 4.0), (T.hb[:, NT:L], 1.0), (T.cf[:, W:L], 0.0)]
    fills += [(T.cf[:, j:j + 1], float(POLY[W - 1 - j])) for j in range(W)]
    for ap, val in fills:
        v.memset(ap, val).then_inc(S.vc, 1)
    nc = len(fills)
    v.wait_ge(S.vc, nc)
    v.tensor_tensor_scan(T.ta[:, 0:NT], T.hb[:, 0:NT], T.d1[:, 0:NT], 1.0, A.mult, A.add).then_inc(S.vc, 1)
    nc += 1

    ne = _n(off)
    parts = [(S.in_e1, 2), (S.in_e2, 3), (S.in_bb, 0), (S.in_l1, 4), (S.in_l2, 5), (S.in_c, 1)]
    v.wait_ge(S.ld3, ld3)
    for i, (sem, j) in enumerate(parts):
        v.wait_ge(sem, ne)
        if i == 0:
            v.tensor_tensor(T.acc[:, :], _blk(T.gb, slot[rk(t)]), _blk(T.rx, j), A.add).then_inc(S.va, 1)
        else:
            v.wait_ge(S.va, i)
            v.tensor_tensor(T.acc[:, :], T.acc[:, :], _blk(T.rx, j), A.add).then_inc(S.va, 1)

    ss = T.nb[:, 3:4]
    g.scalar.wait_ge(S.va, len(parts))
    g.scalar.activation(T.yo[:, :], T.acc[:, :], ActivationFunctionType.Square, scale=1.0 / bound,
                        accum_out=ss).then_inc(S.sq, 1)

    g.wait_ge(S.sq, 1)
    g.remote_dma_fused([
        RemoteDMATransfer(dst_ids=[_dst(topo, kc[0], t)], dma_engine_mask=off, remote_sem=S.k_n, src=ss, dst=T.nb[:, 1:2]),
        RemoteDMATransfer(dst_ids=[_dst(topo, k[0], t)], dma_engine_mask=M["on_all"], remote_sem=S.k_n, src=ss,
                          dst=T.nb[:, 0:1]),
    ], local_sem=S.sent)
    sent += _n(off) + _n(M["on_all"])
    sent += send(b, T.nb[:, 4:5], ss, S.in_nb, off)
    g.wait_ge(S.in_nb, _n(off))
    sent += send(c, T.nb[:, 5:7], T.nb[:, 3:5], S.in_n, off)

    x = T.sm[:, 14:15]
    v.wait_ge(S.sq, 1)
    v.wait_ge(S.vc, nc)
    v.wait_ge(S.in_nb, _n(off))
    v.wait_ge(S.in_n, 3 * _n(off))
    v.tensor_tensor_scan(sc, T.nb[:, 4:11], cst, ss, A.add, A.max).then_inc(S.vx, 1)
    v.wait_ge(S.vx, 1)
    v.tensor_scalar(T.hb[:, 0:NT], T.ta[:, 0:NT], x, 0.25, A.is_gt, A.max).then_inc(S.vx, 1)
    v.wait_ge(S.vx, 2)
    v.tensor_tensor_scan(T.ob[:, 0:L], T.hb[:, 0:L], T.d1[:, 0:L], x, A.mult, A.add).then_inc(S.vx, 1)
    v.tensor_scalar(T.ob[:, L:L + NT], T.hb[:, 0:NT], 0.5, None, A.max).then_inc(S.vx, 1)
    v.wait_ge(S.vx, 4)
    v.tensor_tensor_scan(T.rb[:, 0:L], T.ob[:, NT:NT + L], T.cf[:, 0:L], float(POLY[W]), A.mult, A.add).then_inc(S.vx, 1)
    v.wait_ge(S.vx, 5)
    v.tensor_scalar(T.yo[:, :], T.acc[:, :], T.rb[:, L - 1:L], None, A.mult).then_inc(S.vy, 1)

    g.sync.wait_ge(S.vy, 1)
    g.sync.dma_start(T.y[:, :], T.yo[:, :]).then_inc(S.st, 16)
    g.wait_ge(S.sent, sent)
    g.wait_ge(S.st, 16)


def rank_program(g, core, T, topo):
    P = _plan(T, topo)
    if core in P:
        _rank(g, core, T, topo, P)
        return
    for u in P:
        for i, x in enumerate(P[u]["k"]):
            if x == core:
                _helper(g, core, u, i, T, topo, P)
                return
